import numpy as np
import ml_dtypes


def mxq(x, axis, fmt="e4m3"):
    dtype, down = {"e4m3": (ml_dtypes.float8_e4m3fn, 7), "e5m2": (ml_dtypes.float8_e5m2, 14)}[fmt]
    v = np.moveaxis(np.asarray(x, np.float32).astype(ml_dtypes.bfloat16).astype(np.float64), axis, -1)
    blocks = v.reshape(v.shape[:-1] + (-1, 32))
    amax = np.abs(blocks).max(-1, keepdims=True)
    byte = np.maximum(np.where(amax > 0, np.frexp(amax)[1] - 1 + 127, 0) - down, 1)
    scale = np.exp2(byte - 127.0)
    codes = (blocks / scale).astype(np.float32).astype(dtype).astype(np.float64)
    return np.moveaxis((codes * scale).reshape(v.shape), -1, axis)


WIDE = False


def mx_kscale(k):
    if not WIDE:
        return np.ones(k)
    levels = np.array([10, -10, 5, -5, 0])
    if k % 512:
        return np.exp2(np.random.permutation(np.resize(levels, k // 32))).repeat(32)
    a = np.empty((k // 512, 16))
    for p in range(k // 512):
        a[p, :8] = np.random.permutation(np.resize(levels, 8))
        for g in range(8):
            far = levels[np.abs(levels - a[p, g]) >= 10]
            a[p, g + 8] = far[np.random.randint(len(far))]
    return np.exp2(a.ravel()).repeat(32)


def f64(x):
    return np.asarray(x).astype(np.float64)


def striped(idx):
    return np.tile(idx.reshape(-1, 16).T, (8, 1)).astype(np.uint16)


def unstriped(offs):
    return offs[:16].T.reshape(-1).astype(np.int64)


def striped8(idx):
    return np.concatenate([x.reshape(-1, 16).T for x in idx]).astype(np.uint16)


def runs(offs, k):
    lists = np.stack([offs[16 * r : 16 * r + 16].T.reshape(-1) for r in range(8)]).astype(np.int64)
    return lists[np.arange(k) % 512 // 64]


def pack_weight(w):
    k, n = w.shape
    w = f64(np.asarray(w, np.float32).astype(ml_dtypes.bfloat16)).reshape(k // 32, 32, n)
    amax = np.abs(w).max(1)
    byte = np.clip(np.where(amax > 0, np.frexp(amax)[1] - 1 + 127 - 7, 1), 1, 254)
    scaled = (w * np.exp2(127.0 - byte)[:, None, :]).reshape(k, n).astype(np.float32)
    words = np.ascontiguousarray(scaled.reshape(k // 512, 128, 4, n).transpose(0, 1, 3, 2)).astype(ml_dtypes.float8_e4m3fn).view(np.uint8)
    return words, np.ascontiguousarray(byte.astype(np.uint8).reshape(k // 512, 16, n))


def unpack_weight(words, scales):
    g, p, n, _ = words.shape
    vals = np.ascontiguousarray(words).view(ml_dtypes.float8_e4m3fn).astype(np.float64) * np.repeat(np.exp2(scales.astype(np.float64) - 127.0), 8, axis=1)[..., None]
    return vals.transpose(0, 1, 3, 2).reshape(g * 512, n)


K, T, S, H, C = 512, 2048, 512, 512, 512


def setup_inputs():
    n = np.random.standard_normal
    s = mx_kscale(K)[:, None]
    packed_xT = pack_weight(n((K, T)) * s)
    return {
        "x_words": packed_xT[0],
        "x_scales": packed_xT[1],
        "w1": (n((K, H)) / np.sqrt(K) / s).astype(np.float32),
        "gs": (np.random.uniform(0.5, 1.5, (K, 1)) / s).astype(np.float32),
        "offs": striped(np.random.permutation(T)[:S]),
        "n1": striped8(np.stack([np.random.permutation(S) for _ in range(8)])),
        "n2": striped8(np.stack([np.random.permutation(S) for _ in range(8)])),
        "cand": striped(np.random.permutation(T)[:C]),
        "n3": striped8(np.stack([np.random.permutation(S) for _ in range(8)])),
        "n4": striped8(np.stack([np.random.permutation(S) for _ in range(8)])),
    }


def reference(x_words, x_scales, w1, gs, offs, n1, n2, cand, n3, n4):
    x_cand = unpack_weight(x_words, x_scales)[:, unstriped(cand)]
    xq = unpack_weight(x_words, x_scales)[:, unstriped(offs)]
    y = mxq(f64(w1), 0, "e4m3").T @ xq
    sq = (y) ** 2
    z = f64(gs) * ((y[np.arange(H)[:, None], runs(n2, H)]) / (np.sqrt(sq + sq[np.arange(H)[:, None], runs(n1, H)] + 0.25)))
    s = 0.0625 * ((x_cand.T @ mxq(z, 0, "e4m3")))
    return (s * (s[np.arange(C)[:, None], runs(n3, C)])) * (np.tanh(s[np.arange(C)[:, None], runs(n4, C)]))

@@ -1,0 +1,212 @@
+from contextlib import ExitStack
+
+import concourse.mybir as mybir
+
+K, T, S, H, C = 512, 2048, 512, 512, 512
+FLOPS = 2 * K * H * S + 2 * K * C * S
+
+F32 = mybir.dt.float32
+BF16 = mybir.dt.bfloat16
+I32 = mybir.dt.int32
+U32 = mybir.dt.uint32
+U16 = mybir.dt.uint16
+U8 = mybir.dt.uint8
+FP8X4 = mybir.dt.float8_e4m3fn_x4
+ACT = mybir.ActivationFunctionType
+ALU = mybir.AluOpType
+
+P = 128
+PACK = 4
+HALF = S // 2
+LIST_COLS = S // 16
+
+
+def tile_picked_candrmscube_none_p_kernel(tc, x_words, x_scales, w1, gs, offs, n1, n2, cand, n3, n4, out):
+    nc = tc.nc
+    with ExitStack() as ctx:
+        lists = ctx.enter_context(tc.tile_pool(name="lists", bufs=1))
+        sb = ctx.enter_context(tc.tile_pool(name="sb", bufs=1))
+        ps = ctx.enter_context(tc.psum_pool(name="ps", bufs=1))
+
+        def load_list(name, src):
+            tile = lists.tile([P, LIST_COLS], U16, name=name)
+            nc.sync.dma_start(tile[:], src)
+            return tile
+
+        def half_list(tile, h):
+            return tile[:, h * (LIST_COLS // 2) : (h + 1) * (LIST_COLS // 2)]
+
+        table_bytes = sb.tile([P, T], U8, name="table_bytes")
+        nc.vector.memset(table_bytes[:].bitcast(I32), 0)
+        offs_t = load_list("offs_t", offs)
+        cand_t = load_list("cand_t", cand)
+        n1_t = load_list("n1_t", n1)
+        n2_t = load_list("n2_t", n2)
+        n3_t = load_list("n3_t", n3)
+        w_rows = w1.rearrange("(p j) c -> p j c", j=PACK)
+        w_raw = []
+        for h in range(2):
+            raw = sb.tile([P, PACK, H // 2], F32, name=f"w_raw{h}")
+            nc.sync.dma_start(raw[:], w_rows[:, :, h * (H // 2) : (h + 1) * (H // 2)])
+            w_raw.append(raw)
+        n4_t = load_list("n4_t", n4)
+        for q in range(4):
+            nc.sync.dma_start(table_bytes[32 * q : 32 * q + 4, :].bitcast(I32), x_scales[0, 4 * q : 4 * q + 4, :].bitcast(I32))
+        table_words = sb.tile([P, T], U32, name="table_words")
+        nc.sync.dma_start(table_words[:].bitcast(I32), x_words[0].rearrange("p n r -> p (n r)").bitcast(I32))
+        gs_t = sb.tile([P, PACK], F32, name="gs_t")
+        nc.gpsimd.dma_start(gs_t[:], gs.rearrange("(p t) o -> p (t o)", t=PACK))
+
+        quarter = sb.tile([P, 1], F32, name="quarter")
+        nc.vector.memset(quarter[:], 0.25)
+        warm = sb.tile([P, 2], F32, name="warm")
+        nc.scalar.activation(warm[:, 0:1], quarter[:], ACT.Abs_reciprocal_sqrt, bias=quarter[:])
+
+        y_win = [sb.tile([P, 2 * S], F32, name=f"y_win{t}") for t in range(PACK)]
+        sq_win = [sb.tile([P, 2 * S], F32, name=f"sq_win{t}") for t in range(PACK)]
+        for t in range(PACK):
+            nc.vector.memset(sq_win[t][:, S:], 0.0)
+
+        tok_bytes = sb.tile([P, S], U8, name="tok_bytes", align_bytes=64)
+        nc.vector.tensor_copy(tok_bytes[:], table_bytes[:].indirect(offs_t[:]))
+        cand_bytes_listed = sb.tile([P, C], U8, name="cand_bytes_listed")
+        nc.vector.tensor_copy(cand_bytes_listed[:], table_bytes[:].indirect(cand_t[:]))
+        cand_bytes = sb.tile([P, C], U8, name="cand_bytes", align_bytes=64)
+        nc.vector.tensor_copy(
+            cand_bytes[:].rearrange("p (t m) -> p m t", t=PACK),
+            cand_bytes_listed[:].rearrange("p (m t) -> p m t", t=PACK),
+        )
+
+        w16 = sb.tile([P, PACK, P, PACK], BF16, name="w16", align_bytes=64)
+        for h in range(2):
+            nc.scalar.copy(
+                w16[:, :, 64 * h : 64 * (h + 1), :].rearrange("p t m j -> p m t j"),
+                w_raw[h][:].rearrange("p j (m t) -> p m t j", t=PACK),
+            )
+        w_words = sb.tile([P, H], U32, name="w_words", align_bytes=64)
+        w_bytes = sb.tile([P, H], U8, name="w_bytes", align_bytes=64)
+        nc.vector.quantize_mx(w_words[:].bitcast(FP8X4), w_bytes[:], w16[:].rearrange("p t m j -> p (t m j)"))
+
+        y_ps = [ps.tile([P, S], F32, name=f"y_ps{t}") for t in range(PACK)]
+        for h in range(2):
+            places = slice(h * HALF, (h + 1) * HALF)
+            tok_words = sb.tile([P, HALF], U32, name=f"tok_words{h}", align_bytes=64)
+            nc.vector.tensor_copy(tok_words[:], table_words[:].indirect(half_list(offs_t, h)))
+            for t in range(PACK):
+                cols = slice(t * P, (t + 1) * P)
+                nc.tensor.matmul_mx(y_ps[t][:, places], lhsT=w_words[:, cols].bitcast(FP8X4), lhsT_scale=w_bytes[:, cols], rhs=tok_words[:].bitcast(FP8X4), rhs_scale=tok_bytes[:, places], start=True, stop=True)
+        cand_words = sb.tile([P, C], U32, name="cand_words", align_bytes=64)
+        nc.vector.tensor_copy(cand_words[:].rearrange("p (t m) -> p m t", t=PACK), table_words[:].indirect(cand_t[:]))
+
+        den = [sb.tile([P, S], F32, name=f"den{t}") for t in range(PACK)]
+        inv = [sb.tile([P, S], F32, name=f"inv{t}") for t in range(PACK)]
+        z32 = [sb.tile([P, PACK, HALF], F32, name=f"z32_{h}") for h in range(2)]
+
+        def square(t):
+            nc.scalar.activation(sq_win[t][:, :S], y_ps[t][:], ACT.Square)
+
+        def square_again(t):
+            nc.scalar.activation(y_win[t][:, S:], y_ps[t][:], ACT.Square)
+
+        def gained(t):
+            nc.scalar.activation(y_win[t][:, :S], y_ps[t][:], ACT.Copy, scale=gs_t[:, t : t + 1])
+
+        def add_squares(t):
+            nc.vector.tensor_tensor(den[t][:], sq_win[t][:].indirect(n1_t[:]), y_win[t][:, S:], ALU.add)
+
+        def inverse_root(t):
+            nc.scalar.activation(inv[t][:], den[t][:], ACT.Abs_reciprocal_sqrt, bias=quarter[:])
+
+        def normalise(t, h):
+            nc.vector.tensor_tensor(z32[h][:, t, :], y_win[t][:].indirect(half_list(n2_t, h)), inv[t][:, h * HALF : (h + 1) * HALF], ALU.mult)
+
+        square(0)
+        nc.vector.tensor_copy(y_win[0][:, S:], sq_win[0][:, :S])
+        add_squares(0)
+        square(1)
+        square_again(1)
+        add_squares(1)
+        gained(0)
+        inverse_root(0)
+        normalise(0, 0)
+        normalise(0, 1)
+        square(2)
+        square_again(2)
+        add_squares(2)
+        inverse_root(1)
+        gained(1)
+        normalise(1, 0)
+        normalise(1, 1)
+        square(3)
+        square_again(3)
+        add_squares(3)
+        inverse_root(2)
+        gained(2)
+        gained(3)
+        inverse_root(3)
+
+        z16 = [sb.tile([P, HALF, PACK], BF16, name=f"z16_{h}", align_bytes=64) for h in range(2)]
+        z_words = [sb.tile([P, HALF], U32, name=f"z_words{h}", align_bytes=64) for h in range(2)]
+        z_bytes = [sb.tile([P, HALF], U8, name=f"z_bytes{h}", align_bytes=64) for h in range(2)]
+        s_ps = [ps.tile([P, S], F32, name=f"s_ps{t}") for t in range(PACK)]
+
+        def interleave(copy, h):
+            copy(
+                z16[h][:].rearrange("p (c i) t -> p c t i", i=4),
+                z32[h][:].rearrange("p t (c i) -> p c t i", i=4),
+            )
+
+        def quantise_and_score(h):
+            nc.vector.quantize_mx(z_words[h][:].bitcast(FP8X4), z_bytes[h][:], z16[h][:].rearrange("p c t -> p (c t)"))
+            for t in range(PACK):
+                cols = slice(t * P, (t + 1) * P)
+                nc.tensor.matmul_mx(s_ps[t][:, h * HALF : (h + 1) * HALF], lhsT=cand_words[:, cols].bitcast(FP8X4), lhsT_scale=cand_bytes[:, cols], rhs=z_words[h][:].bitcast(FP8X4), rhs_scale=z_bytes[h][:], start=True, stop=True)
+
+        normalise(2, 0)
+        normalise(3, 0)
+        interleave(nc.scalar.copy, 0)
+        nc.scalar.activation(warm[:, 1:2], z16[0][:, 0, 0:1], ACT.Sigmoid)
+        normalise(2, 1)
+        normalise(3, 1)
+        quantise_and_score(0)
+        interleave(nc.vector.tensor_copy, 1)
+        quantise_and_score(1)
+
+        out_rows = out.rearrange("(p t) n -> t p n", t=PACK)
+        s_win = sq_win
+        sig = [sb.tile([P, S], F32, name=f"sig{t}") for t in range(PACK)]
+        prod = [sb.tile([P, S], F32, name=f"prod{t}") for t in range(PACK)]
+        res = [sb.tile([P, S], F32, name=f"res{t}") for t in range(PACK)]
+
+        def sigmoid(t):
+            nc.scalar.activation(sig[t][:], s_win[t][:].indirect(n4_t[:]), ACT.Sigmoid, scale=16.0)
+
+        def gate(t):
+            nc.vector.scalar_tensor_tensor(prod[t][:], sig[t][:], 0.5, s_ps[t][:], ALU.subtract, ALU.mult)
+
+        def finish(t, pieces):
+            if pieces == 1:
+                nc.vector.tensor_tensor(res[t][:], s_win[t][:].indirect(n3_t[:]), prod[t][:], ALU.mult)
+                nc.sync.dma_start(out_rows[t], res[t][:])
+            else:
+                for h in range(2):
+                    cols = slice(h * HALF, (h + 1) * HALF)
+                    nc.vector.tensor_tensor(res[t][:, cols], s_win[t][:].indirect(half_list(n3_t, h)), prod[t][:, cols], ALU.mult)
+                    nc.sync.dma_start(out_rows[t][:, cols], res[t][:, cols])
+
+        nc.scalar.activation(s_win[0][:, :S], s_ps[0][:], ACT.Copy, scale=1.0 / 128)
+        nc.vector.tensor_scalar(s_win[1][:, :S], s_ps[1][:], 1.0 / 128, None, ALU.mult)
+        nc.vector.tensor_scalar(s_win[2][:, :S], s_ps[2][:], 1.0 / 128, None, ALU.mult)
+        sigmoid(0)
+        gate(0)
+        finish(0, 1)
+        sigmoid(1)
+        gate(1)
+        sigmoid(2)
+        gate(2)
+        finish(1, 1)
+        nc.scalar.activation(s_win[3][:, :S], s_ps[3][:], ACT.Copy, scale=1.0 / 128)
+        sigmoid(3)
+        gate(3)
+        finish(2, 1)
+        finish(3, 2)

@@ -33,34 +33,35 @@ def tile_picked_candrmscube_none_p_kernel(tc, x_words, x_scales, w1, gs, offs, n
             nc.sync.dma_start(tile[:], src)
             return tile
 
-        def half_list(tile, h):
-            return tile[:, h * (LIST_COLS // 2) : (h + 1) * (LIST_COLS // 2)]
+        whole = [(slice(0, S), slice(0, LIST_COLS))]
+        halves = [(slice(h * HALF, (h + 1) * HALF), slice(h * LIST_COLS // 2, (h + 1) * LIST_COLS // 2)) for h in range(2)]
 
-        table_bytes = sb.tile([P, T], U8, name="table_bytes")
-        nc.vector.memset(table_bytes[:].bitcast(I32), 0)
+        table_bytes = sb.tile([P, T], U8, name="table_bytes", tag="table_bytes", align_bytes=64)
+        nc.vector.memset(table_bytes[:, : T // 2].bitcast(I32), 0)
+        nc.gpsimd.memset(table_bytes[:, T // 2 :].bitcast(I32), 0)
+        for q in range(4):
+            nc.scalar.dma_start(table_bytes[32 * q : 32 * q + 4, :].bitcast(I32), x_scales[0, 4 * q : 4 * q + 4, :].bitcast(I32))
         offs_t = load_list("offs_t", offs)
-        cand_t = load_list("cand_t", cand)
-        n1_t = load_list("n1_t", n1)
-        n2_t = load_list("n2_t", n2)
-        n3_t = load_list("n3_t", n3)
         w_rows = w1.rearrange("(p j) c -> p j c", j=PACK)
         w_raw = []
         for h in range(2):
             raw = sb.tile([P, PACK, H // 2], F32, name=f"w_raw{h}")
             nc.sync.dma_start(raw[:], w_rows[:, :, h * (H // 2) : (h + 1) * (H // 2)])
             w_raw.append(raw)
-        n4_t = load_list("n4_t", n4)
-        for q in range(4):
-            nc.sync.dma_start(table_bytes[32 * q : 32 * q + 4, :].bitcast(I32), x_scales[0, 4 * q : 4 * q + 4, :].bitcast(I32))
+        quarter = sb.tile([P, 1], F32, name="quarter")
+        nc.vector.memset(quarter[:], 0.25)
+        warm_root = sb.tile([P, 1], F32, name="warm_root")
+        nc.scalar.activation(warm_root[:], quarter[:], ACT.Abs_reciprocal_sqrt, bias=quarter[:])
+        cand_t = load_list("cand_t", cand)
         table_words = sb.tile([P, T], U32, name="table_words")
         nc.sync.dma_start(table_words[:].bitcast(I32), x_words[0].rearrange("p n r -> p (n r)").bitcast(I32))
+        n1_t = load_list("n1_t", n1)
+        n2_t = load_list("n2_t", n2)
+        n3_t = load_list("n3_t", n3)
+        n4_t = load_list("n4_t", n4)
         gs_t = sb.tile([P, PACK], F32, name="gs_t")
         nc.gpsimd.dma_start(gs_t[:], gs.rearrange("(p t) o -> p (t o)", t=PACK))
 
-        quarter = sb.tile([P, 1], F32, name="quarter")
-        nc.vector.memset(quarter[:], 0.25)
-        warm = sb.tile([P, 2], F32, name="warm")
-        nc.scalar.activation(warm[:, 0:1], quarter[:], ACT.Abs_reciprocal_sqrt, bias=quarter[:])
 
         y_win = [sb.tile([P, 2 * S], F32, name=f"y_win{t}") for t in range(PACK)]
         sq_win = [sb.tile([P, 2 * S], F32, name=f"sq_win{t}") for t in range(PACK)]
@@ -71,11 +72,6 @@ def tile_picked_candrmscube_none_p_kernel(tc, x_words, x_scales, w1, gs, offs, n
         nc.vector.tensor_copy(tok_bytes[:], table_bytes[:].indirect(offs_t[:]))
         cand_bytes_listed = sb.tile([P, C], U8, name="cand_bytes_listed")
         nc.vector.tensor_copy(cand_bytes_listed[:], table_bytes[:].indirect(cand_t[:]))
-        cand_bytes = sb.tile([P, C], U8, name="cand_bytes", align_bytes=64)
-        nc.vector.tensor_copy(
-            cand_bytes[:].rearrange("p (t m) -> p m t", t=PACK),
-            cand_bytes_listed[:].rearrange("p (m t) -> p m t", t=PACK),
-        )
 
         w16 = sb.tile([P, PACK, P, PACK], BF16, name="w16", align_bytes=64)
         for h in range(2):
@@ -83,24 +79,33 @@ def tile_picked_candrmscube_none_p_kernel(tc, x_words, x_scales, w1, gs, offs, n
                 w16[:, :, 64 * h : 64 * (h + 1), :].rearrange("p t m j -> p m t j"),
                 w_raw[h][:].rearrange("p j (m t) -> p m t j", t=PACK),
             )
-        w_words = sb.tile([P, H], U32, name="w_words", align_bytes=64)
+        w_words = sb.tile([P, H], U32, name="w_words", tag="table_bytes", align_bytes=64)
         w_bytes = sb.tile([P, H], U8, name="w_bytes", align_bytes=64)
         nc.vector.quantize_mx(w_words[:].bitcast(FP8X4), w_bytes[:], w16[:].rearrange("p t m j -> p (t m j)"))
 
         y_ps = [ps.tile([P, S], F32, name=f"y_ps{t}") for t in range(PACK)]
-        for h in range(2):
-            places = slice(h * HALF, (h + 1) * HALF)
-            tok_words = sb.tile([P, HALF], U32, name=f"tok_words{h}", align_bytes=64)
-            nc.vector.tensor_copy(tok_words[:], table_words[:].indirect(half_list(offs_t, h)))
-            for t in range(PACK):
-                cols = slice(t * P, (t + 1) * P)
-                nc.tensor.matmul_mx(y_ps[t][:, places], lhsT=w_words[:, cols].bitcast(FP8X4), lhsT_scale=w_bytes[:, cols], rhs=tok_words[:].bitcast(FP8X4), rhs_scale=tok_bytes[:, places], start=True, stop=True)
+        tok_words = sb.tile([P, S], U32, name="tok_words", align_bytes=64)
+        for cols, entries in halves:
+            nc.vector.tensor_copy(tok_words[:, cols], table_words[:].indirect(offs_t[:, entries]))
+
+        def product(bank, t, lhs_words, lhs_bytes, rhs_words, rhs_bytes):
+            rows = slice(t * P, (t + 1) * P)
+            for cols, entries in halves if t == 0 else whole:
+                nc.tensor.matmul_mx(bank[:, cols], lhsT=lhs_words[:, rows].bitcast(FP8X4), lhsT_scale=lhs_bytes[:, rows], rhs=rhs_words[:, cols].bitcast(FP8X4), rhs_scale=rhs_bytes[:, cols], start=True, stop=True)
+
+        for t in range(PACK):
+            product(y_ps[t], t, w_words, w_bytes, tok_words, tok_bytes)
+        cand_bytes = sb.tile([P, C], U8, name="cand_bytes", align_bytes=64)
+        nc.vector.tensor_copy(
+            cand_bytes[:].rearrange("p (t m) -> p m t", t=PACK),
+            cand_bytes_listed[:].rearrange("p (m t) -> p m t", t=PACK),
+        )
         cand_words = sb.tile([P, C], U32, name="cand_words", align_bytes=64)
         nc.vector.tensor_copy(cand_words[:].rearrange("p (t m) -> p m t", t=PACK), table_words[:].indirect(cand_t[:]))
 
         den = [sb.tile([P, S], F32, name=f"den{t}") for t in range(PACK)]
         inv = [sb.tile([P, S], F32, name=f"inv{t}") for t in range(PACK)]
-        z32 = [sb.tile([P, PACK, HALF], F32, name=f"z32_{h}") for h in range(2)]
+        z32 = sb.tile([P, PACK, S], F32, name="z32")
 
         def square(t):
             nc.scalar.activation(sq_win[t][:, :S], y_ps[t][:], ACT.Square)
@@ -117,60 +122,60 @@ def tile_picked_candrmscube_none_p_kernel(tc, x_words, x_scales, w1, gs, offs, n
         def inverse_root(t):
             nc.scalar.activation(inv[t][:], den[t][:], ACT.Abs_reciprocal_sqrt, bias=quarter[:])
 
-        def normalise(t, h):
-            nc.vector.tensor_tensor(z32[h][:, t, :], y_win[t][:].indirect(half_list(n2_t, h)), inv[t][:, h * HALF : (h + 1) * HALF], ALU.mult)
+        def normalise(t, pieces):
+            for cols, entries in pieces:
+                nc.vector.tensor_tensor(z32[:, t, cols], y_win[t][:].indirect(n2_t[:, entries]), inv[t][:, cols], ALU.mult)
 
         square(0)
-        nc.vector.tensor_copy(y_win[0][:, S:], sq_win[0][:, :S])
+        square_again(0)
         add_squares(0)
         square(1)
         square_again(1)
         add_squares(1)
         gained(0)
         inverse_root(0)
-        normalise(0, 0)
-        normalise(0, 1)
+        normalise(0, whole)
         square(2)
         square_again(2)
         add_squares(2)
         inverse_root(1)
         gained(1)
-        normalise(1, 0)
-        normalise(1, 1)
+        normalise(1, whole)
         square(3)
         square_again(3)
         add_squares(3)
         inverse_root(2)
         gained(2)
+        normalise(2, whole)
         gained(3)
         inverse_root(3)
 
         z16 = [sb.tile([P, HALF, PACK], BF16, name=f"z16_{h}", align_bytes=64) for h in range(2)]
-        z_words = [sb.tile([P, HALF], U32, name=f"z_words{h}", align_bytes=64) for h in range(2)]
-        z_bytes = [sb.tile([P, HALF], U8, name=f"z_bytes{h}", align_bytes=64) for h in range(2)]
-        s_ps = [ps.tile([P, S], F32, name=f"s_ps{t}") for t in range(PACK)]
+        z_words = sb.tile([P, S], U32, name="z_words", align_bytes=64)
+        z_bytes = sb.tile([P, S], U8, name="z_bytes", align_bytes=64)
+        s_ps = [ps.tile([P, S], F32, name=f"s_ps{t}") for t in range(PACK - 1)]
 
         def interleave(copy, h):
             copy(
                 z16[h][:].rearrange("p (c i) t -> p c t i", i=4),
-                z32[h][:].rearrange("p t (c i) -> p c t i", i=4),
+                z32[:, :, h * HALF : (h + 1) * HALF].rearrange("p t (c i) -> p c t i", i=4),
             )
 
-        def quantise_and_score(h):
-            nc.vector.quantize_mx(z_words[h][:].bitcast(FP8X4), z_bytes[h][:], z16[h][:].rearrange("p c t -> p (c t)"))
-            for t in range(PACK):
-                cols = slice(t * P, (t + 1) * P)
-                nc.tensor.matmul_mx(s_ps[t][:, h * HALF : (h + 1) * HALF], lhsT=cand_words[:, cols].bitcast(FP8X4), lhsT_scale=cand_bytes[:, cols], rhs=z_words[h][:].bitcast(FP8X4), rhs_scale=z_bytes[h][:], start=True, stop=True)
+        def quantise(h):
+            nc.vector.quantize_mx(z_words[:, halves[h][0]].bitcast(FP8X4), z_bytes[:, halves[h][0]], z16[h][:].rearrange("p c t -> p (c t)"))
 
-        normalise(2, 0)
-        normalise(3, 0)
+        normalise(3, halves[:1])
         interleave(nc.scalar.copy, 0)
-        nc.scalar.activation(warm[:, 1:2], z16[0][:, 0, 0:1], ACT.Sigmoid)
-        normalise(2, 1)
-        normalise(3, 1)
-        quantise_and_score(0)
+        normalise(3, halves[1:])
         interleave(nc.vector.tensor_copy, 1)
-        quantise_and_score(1)
+        quantise(0)
+        quantise(1)
+
+        def score(t):
+            product(s_ps[t], t, cand_words, cand_bytes, z_words, z_bytes)
+
+        for t in range(PACK - 1):
+            score(t)
 
         out_rows = out.rearrange("(p t) n -> t p n", t=PACK)
         s_win = sq_win
@@ -178,35 +183,35 @@ def tile_picked_candrmscube_none_p_kernel(tc, x_words, x_scales, w1, gs, offs, n
         prod = [sb.tile([P, S], F32, name=f"prod{t}") for t in range(PACK)]
         res = [sb.tile([P, S], F32, name=f"res{t}") for t in range(PACK)]
 
-        def sigmoid(t):
-            nc.scalar.activation(sig[t][:], s_win[t][:].indirect(n4_t[:]), ACT.Sigmoid, scale=16.0)
+        def sigmoid(t, pieces):
+            for cols, entries in pieces:
+                nc.scalar.activation(sig[t][:, cols], s_win[t][:].indirect(n4_t[:, entries]), ACT.Sigmoid, scale=16.0)
 
-        def gate(t):
-            nc.vector.scalar_tensor_tensor(prod[t][:], sig[t][:], 0.5, s_ps[t][:], ALU.subtract, ALU.mult)
+        def gate(t, pieces):
+            for cols, entries in pieces:
+                nc.vector.scalar_tensor_tensor(prod[t][:, cols], sig[t][:, cols], 0.5, s_ps[t][:, cols], ALU.subtract, ALU.mult)
 
         def finish(t, pieces):
-            if pieces == 1:
-                nc.vector.tensor_tensor(res[t][:], s_win[t][:].indirect(n3_t[:]), prod[t][:], ALU.mult)
-                nc.sync.dma_start(out_rows[t], res[t][:])
-            else:
-                for h in range(2):
-                    cols = slice(h * HALF, (h + 1) * HALF)
-                    nc.vector.tensor_tensor(res[t][:, cols], s_win[t][:].indirect(half_list(n3_t, h)), prod[t][:, cols], ALU.mult)
-                    nc.sync.dma_start(out_rows[t][:, cols], res[t][:, cols])
+            for cols, entries in pieces:
+                nc.vector.tensor_tensor(res[t][:, cols], s_win[t][:].indirect(n3_t[:, entries]), prod[t][:, cols], ALU.mult)
+                nc.sync.dma_start(out_rows[t][:, cols], res[t][:, cols])
 
-        nc.scalar.activation(s_win[0][:, :S], s_ps[0][:], ACT.Copy, scale=1.0 / 128)
+        nc.vector.tensor_scalar(s_win[0][:, :S], s_ps[0][:], 1.0 / 128, None, ALU.mult)
         nc.vector.tensor_scalar(s_win[1][:, :S], s_ps[1][:], 1.0 / 128, None, ALU.mult)
         nc.vector.tensor_scalar(s_win[2][:, :S], s_ps[2][:], 1.0 / 128, None, ALU.mult)
-        sigmoid(0)
-        gate(0)
-        finish(0, 1)
-        sigmoid(1)
-        gate(1)
-        sigmoid(2)
-        gate(2)
-        finish(1, 1)
+        sigmoid(0, halves)
+        gate(0, halves)
+        last_bank = ps.tile([P, S], F32, name="last_bank", tag="s_ps0")
+        s_ps.append(last_bank)
+        score(3)
+        finish(0, halves)
+        sigmoid(1, whole)
+        gate(1, whole)
+        sigmoid(2, whole)
+        gate(2, whole)
+        finish(1, whole)
         nc.scalar.activation(s_win[3][:, :S], s_ps[3][:], ACT.Copy, scale=1.0 / 128)
-        sigmoid(3)
-        gate(3)
-        finish(2, 1)
-        finish(3, 2)
+        sigmoid(3, whole)
+        gate(3, whole)
+        finish(2, whole)
+        finish(3, halves)

@@ -39,28 +39,26 @@ def tile_picked_candrmscube_none_p_kernel(tc, x_words, x_scales, w1, gs, offs, n
         table_bytes = sb.tile([P, T], U8, name="table_bytes", tag="table_bytes", align_bytes=64)
         nc.vector.memset(table_bytes[:, : T // 2].bitcast(I32), 0)
         nc.gpsimd.memset(table_bytes[:, T // 2 :].bitcast(I32), 0)
-        for q in range(4):
-            nc.scalar.dma_start(table_bytes[32 * q : 32 * q + 4, :].bitcast(I32), x_scales[0, 4 * q : 4 * q + 4, :].bitcast(I32))
-        offs_t = load_list("offs_t", offs)
         w_rows = w1.rearrange("(p j) c -> p j c", j=PACK)
-        w_raw = []
-        for h in range(2):
-            raw = sb.tile([P, PACK, H // 2], F32, name=f"w_raw{h}")
-            nc.sync.dma_start(raw[:], w_rows[:, :, h * (H // 2) : (h + 1) * (H // 2)])
-            w_raw.append(raw)
+        w_raw = [sb.tile([P, PACK, H // 2], F32, name=f"w_raw{h}") for h in range(2)]
+        offs_t = load_list("offs_t", offs)
+        nc.sync.dma_start(w_raw[0][:], w_rows[:, :, : H // 2])
+        cand_t = load_list("cand_t", cand)
+        n1_t = load_list("n1_t", n1)
+        for q in range(4):
+            nc.sync.dma_start(table_bytes[32 * q : 32 * q + 4, :].bitcast(I32), x_scales[0, 4 * q : 4 * q + 4, :].bitcast(I32))
+        nc.sync.dma_start(w_raw[1][:], w_rows[:, :, H // 2 :])
         quarter = sb.tile([P, 1], F32, name="quarter")
         nc.vector.memset(quarter[:], 0.25)
         warm_root = sb.tile([P, 1], F32, name="warm_root")
         nc.scalar.activation(warm_root[:], quarter[:], ACT.Abs_reciprocal_sqrt, bias=quarter[:])
-        cand_t = load_list("cand_t", cand)
         table_words = sb.tile([P, T], U32, name="table_words")
         nc.sync.dma_start(table_words[:].bitcast(I32), x_words[0].rearrange("p n r -> p (n r)").bitcast(I32))
-        n1_t = load_list("n1_t", n1)
         n2_t = load_list("n2_t", n2)
         n3_t = load_list("n3_t", n3)
         n4_t = load_list("n4_t", n4)
         gs_t = sb.tile([P, PACK], F32, name="gs_t")
-        nc.gpsimd.dma_start(gs_t[:], gs.rearrange("(p t) o -> p (t o)", t=PACK))
+        nc.sync.dma_start(gs_t[:], gs.rearrange("(p t) o -> p (t o)", t=PACK))
 
 
         y_win = [sb.tile([P, 2 * S], F32, name=f"y_win{t}") for t in range(PACK)]
@@ -83,18 +81,21 @@ def tile_picked_candrmscube_none_p_kernel(tc, x_words, x_scales, w1, gs, offs, n
         w_bytes = sb.tile([P, H], U8, name="w_bytes", align_bytes=64)
         nc.vector.quantize_mx(w_words[:].bitcast(FP8X4), w_bytes[:], w16[:].rearrange("p t m j -> p (t m j)"))
 
-        y_ps = [ps.tile([P, S], F32, name=f"y_ps{t}") for t in range(PACK)]
         tok_words = sb.tile([P, S], U32, name="tok_words", align_bytes=64)
         for cols, entries in halves:
             nc.vector.tensor_copy(tok_words[:, cols], table_words[:].indirect(offs_t[:, entries]))
 
-        def product(bank, t, lhs_words, lhs_bytes, rhs_words, rhs_bytes):
+        def product(name, tags, t, lhs_words, lhs_bytes, rhs_words, rhs_bytes):
             rows = slice(t * P, (t + 1) * P)
-            for cols, entries in halves if t == 0 else whole:
-                nc.tensor.matmul_mx(bank[:, cols], lhsT=lhs_words[:, rows].bitcast(FP8X4), lhsT_scale=lhs_bytes[:, rows], rhs=rhs_words[:, cols].bitcast(FP8X4), rhs_scale=rhs_bytes[:, cols], start=True, stop=True)
+            made = []
+            for tag, (cols, entries) in zip(tags, halves if len(tags) == 2 else whole):
+                bank = ps.tile([P, cols.stop - cols.start], F32, name=f"{name}_{tag}", tag=tag)
+                nc.tensor.matmul_mx(bank[:], lhsT=lhs_words[:, rows].bitcast(FP8X4), lhsT_scale=lhs_bytes[:, rows], rhs=rhs_words[:, cols].bitcast(FP8X4), rhs_scale=rhs_bytes[:, cols], start=True, stop=True)
+                made.append((bank, cols))
+            return made
 
-        for t in range(PACK):
-            product(y_ps[t], t, w_words, w_bytes, tok_words, tok_bytes)
+        bank_tags = [["bank0a", "bank0b"], ["bank1"], ["bank2"], ["bank3"]]
+        y_ps = [product("y", bank_tags[t], t, w_words, w_bytes, tok_words, tok_bytes) for t in range(PACK)]
         cand_bytes = sb.tile([P, C], U8, name="cand_bytes", align_bytes=64)
         nc.vector.tensor_copy(
             cand_bytes[:].rearrange("p (t m) -> p m t", t=PACK),
@@ -107,17 +108,18 @@ def tile_picked_candrmscube_none_p_kernel(tc, x_words, x_scales, w1, gs, offs, n
         inv = [sb.tile([P, S], F32, name=f"inv{t}") for t in range(PACK)]
         z32 = sb.tile([P, PACK, S], F32, name="z32")
 
-        def square(t):
-            nc.scalar.activation(sq_win[t][:, :S], y_ps[t][:], ACT.Square)
-
-        def square_again(t):
-            nc.scalar.activation(y_win[t][:, S:], y_ps[t][:], ACT.Square)
+        def squares(t):
+            for bank, cols in y_ps[t]:
+                nc.scalar.activation(sq_win[t][:, cols], bank[:], ACT.Square)
+                nc.scalar.activation(y_win[t][:, S + cols.start : S + cols.stop], bank[:], ACT.Square)
 
         def gained(t):
-            nc.scalar.activation(y_win[t][:, :S], y_ps[t][:], ACT.Copy, scale=gs_t[:, t : t + 1])
+            for bank, cols in y_ps[t]:
+                nc.scalar.activation(y_win[t][:, cols], bank[:], ACT.Copy, scale=gs_t[:, t : t + 1])
 
-        def add_squares(t):
-            nc.vector.tensor_tensor(den[t][:], sq_win[t][:].indirect(n1_t[:]), y_win[t][:, S:], ALU.add)
+        def add_squares(t, pieces):
+            for cols, entries in pieces:
+                nc.vector.tensor_tensor(den[t][:, cols], sq_win[t][:].indirect(n1_t[:, entries]), y_win[t][:, S + cols.start : S + cols.stop], ALU.add)
 
         def inverse_root(t):
             nc.scalar.activation(inv[t][:], den[t][:], ACT.Abs_reciprocal_sqrt, bias=quarter[:])
@@ -126,24 +128,20 @@ def tile_picked_candrmscube_none_p_kernel(tc, x_words, x_scales, w1, gs, offs, n
             for cols, entries in pieces:
                 nc.vector.tensor_tensor(z32[:, t, cols], y_win[t][:].indirect(n2_t[:, entries]), inv[t][:, cols], ALU.mult)
 
-        square(0)
-        square_again(0)
-        add_squares(0)
-        square(1)
-        square_again(1)
-        add_squares(1)
+        squares(0)
+        add_squares(0, halves)
+        squares(1)
+        add_squares(1, whole)
         gained(0)
         inverse_root(0)
         normalise(0, whole)
-        square(2)
-        square_again(2)
-        add_squares(2)
+        squares(2)
+        add_squares(2, whole)
         inverse_root(1)
         gained(1)
         normalise(1, whole)
-        square(3)
-        square_again(3)
-        add_squares(3)
+        squares(3)
+        add_squares(3, whole)
         inverse_root(2)
         gained(2)
         normalise(2, whole)
@@ -153,7 +151,6 @@ def tile_picked_candrmscube_none_p_kernel(tc, x_words, x_scales, w1, gs, offs, n
         z16 = [sb.tile([P, HALF, PACK], BF16, name=f"z16_{h}", align_bytes=64) for h in range(2)]
         z_words = sb.tile([P, S], U32, name="z_words", align_bytes=64)
         z_bytes = sb.tile([P, S], U8, name="z_bytes", align_bytes=64)
-        s_ps = [ps.tile([P, S], F32, name=f"s_ps{t}") for t in range(PACK - 1)]
 
         def interleave(copy, h):
             copy(
@@ -171,11 +168,10 @@ def tile_picked_candrmscube_none_p_kernel(tc, x_words, x_scales, w1, gs, offs, n
         quantise(0)
         quantise(1)
 
-        def score(t):
-            product(s_ps[t], t, cand_words, cand_bytes, z_words, z_bytes)
+        def score(t, tags):
+            return product("s", tags, t, cand_words, cand_bytes, z_words, z_bytes)
 
-        for t in range(PACK - 1):
-            score(t)
+        s_ps = [score(t, bank_tags[t]) for t in range(PACK - 1)]
 
         out_rows = out.rearrange("(p t) n -> t p n", t=PACK)
         s_win = sq_win
@@ -187,31 +183,29 @@ def tile_picked_candrmscube_none_p_kernel(tc, x_words, x_scales, w1, gs, offs, n
             for cols, entries in pieces:
                 nc.scalar.activation(sig[t][:, cols], s_win[t][:].indirect(n4_t[:, entries]), ACT.Sigmoid, scale=16.0)
 
-        def gate(t, pieces):
-            for cols, entries in pieces:
-                nc.vector.scalar_tensor_tensor(prod[t][:, cols], sig[t][:, cols], 0.5, s_ps[t][:, cols], ALU.subtract, ALU.mult)
+        def gate(t):
+            for bank, cols in s_ps[t]:
+                nc.vector.scalar_tensor_tensor(prod[t][:, cols], sig[t][:, cols], 0.5, bank[:], ALU.subtract, ALU.mult)
 
         def finish(t, pieces):
             for cols, entries in pieces:
                 nc.vector.tensor_tensor(res[t][:, cols], s_win[t][:].indirect(n3_t[:, entries]), prod[t][:, cols], ALU.mult)
                 nc.sync.dma_start(out_rows[t][:, cols], res[t][:, cols])
 
-        nc.vector.tensor_scalar(s_win[0][:, :S], s_ps[0][:], 1.0 / 128, None, ALU.mult)
-        nc.vector.tensor_scalar(s_win[1][:, :S], s_ps[1][:], 1.0 / 128, None, ALU.mult)
-        nc.vector.tensor_scalar(s_win[2][:, :S], s_ps[2][:], 1.0 / 128, None, ALU.mult)
+        for t in range(PACK - 1):
+            for bank, cols in s_ps[t]:
+                nc.vector.tensor_scalar(s_win[t][:, cols], bank[:], 1.0 / 128, None, ALU.mult)
         sigmoid(0, halves)
-        gate(0, halves)
-        last_bank = ps.tile([P, S], F32, name="last_bank", tag="s_ps0")
-        s_ps.append(last_bank)
-        score(3)
+        gate(0)
+        s_ps.append(score(3, ["bank0b"]))
         finish(0, halves)
         sigmoid(1, whole)
-        gate(1, whole)
+        gate(1)
         sigmoid(2, whole)
-        gate(2, whole)
+        gate(2)
         finish(1, whole)
-        nc.scalar.activation(s_win[3][:, :S], s_ps[3][:], ACT.Copy, scale=1.0 / 128)
+        nc.scalar.activation(s_win[3][:, :S], s_ps[3][0][0][:], ACT.Copy, scale=1.0 / 128)
         sigmoid(3, whole)
-        gate(3, whole)
+        gate(3)
         finish(2, whole)
-        finish(3, halves)
+        finish(3, [(slice(0, 384), slice(0, 24)), (slice(384, 512), slice(24, 32))])

@@ -17,41 +17,48 @@ ALU = mybir.AluOpType
 
 P = 128
 PACK = 4
+PER_COLUMN = 16
 HALF = S // 2
-LIST_COLS = S // 16
+LAST_PIECE = 128
+
+SCORE_SCALE = 0.0625
+WINDOW_SCALE = 2 * SCORE_SCALE * SCORE_SCALE
+SIGMOID_SCALE = 2 * SCORE_SCALE / WINDOW_SCALE
+
+
+def piece(start, stop):
+    return slice(start, stop), slice(start // PER_COLUMN, stop // PER_COLUMN)
 
 
 def tile_picked_candrmscube_none_p_kernel(tc, x_words, x_scales, w1, gs, offs, n1, n2, cand, n3, n4, out):
     nc = tc.nc
+    whole = [piece(0, S)]
+    halves = [piece(0, HALF), piece(HALF, S)]
+    last = PACK - 1
+
     with ExitStack() as ctx:
         lists = ctx.enter_context(tc.tile_pool(name="lists", bufs=1))
         sb = ctx.enter_context(tc.tile_pool(name="sb", bufs=1))
         ps = ctx.enter_context(tc.psum_pool(name="ps", bufs=1))
 
         def load_list(name, src):
-            tile = lists.tile([P, LIST_COLS], U16, name=name)
+            tile = lists.tile([P, S // PER_COLUMN], U16, name=name)
             nc.sync.dma_start(tile[:], src)
             return tile
-
-        whole = [(slice(0, S), slice(0, LIST_COLS))]
-        halves = [(slice(h * HALF, (h + 1) * HALF), slice(h * LIST_COLS // 2, (h + 1) * LIST_COLS // 2)) for h in range(2)]
 
         table_bytes = sb.tile([P, T], U8, name="table_bytes", tag="table_bytes", align_bytes=64)
         nc.vector.memset(table_bytes[:, : T // 2].bitcast(I32), 0)
         nc.gpsimd.memset(table_bytes[:, T // 2 :].bitcast(I32), 0)
+
         w_rows = w1.rearrange("(p j) c -> p j c", j=PACK)
         w_raw = [sb.tile([P, PACK, H // 2], F32, name=f"w_raw{h}") for h in range(2)]
         offs_t = load_list("offs_t", offs)
         nc.sync.dma_start(w_raw[0][:], w_rows[:, :, : H // 2])
         cand_t = load_list("cand_t", cand)
         n1_t = load_list("n1_t", n1)
-        for q in range(4):
+        for q in range(P // 32):
             nc.sync.dma_start(table_bytes[32 * q : 32 * q + 4, :].bitcast(I32), x_scales[0, 4 * q : 4 * q + 4, :].bitcast(I32))
         nc.sync.dma_start(w_raw[1][:], w_rows[:, :, H // 2 :])
-        quarter = sb.tile([P, 1], F32, name="quarter")
-        nc.vector.memset(quarter[:], 0.25)
-        warm_root = sb.tile([P, 1], F32, name="warm_root")
-        nc.scalar.activation(warm_root[:], quarter[:], ACT.Abs_reciprocal_sqrt, bias=quarter[:])
         table_words = sb.tile([P, T], U32, name="table_words")
         nc.sync.dma_start(table_words[:].bitcast(I32), x_words[0].rearrange("p n r -> p (n r)").bitcast(I32))
         n2_t = load_list("n2_t", n2)
@@ -60,11 +67,15 @@ def tile_picked_candrmscube_none_p_kernel(tc, x_words, x_scales, w1, gs, offs, n
         gs_t = sb.tile([P, PACK], F32, name="gs_t")
         nc.sync.dma_start(gs_t[:], gs.rearrange("(p t) o -> p (t o)", t=PACK))
 
+        sixteen = sb.tile([P, 1], F32, name="sixteen")
+        nc.vector.memset(sixteen[:], 16.0)
+        quarter = sb.tile([P, 1], F32, name="quarter")
+        nc.scalar.activation(quarter[:], sixteen[:], ACT.Abs_reciprocal_sqrt)
 
-        y_win = [sb.tile([P, 2 * S], F32, name=f"y_win{t}") for t in range(PACK)]
-        sq_win = [sb.tile([P, 2 * S], F32, name=f"sq_win{t}") for t in range(PACK)]
+        y_and_sq = [sb.tile([P, 2 * S], F32, name=f"y_and_sq{t}") for t in range(PACK)]
+        lookup = [sb.tile([P, 2 * S], F32, name=f"lookup{t}") for t in range(PACK)]
         for t in range(PACK):
-            nc.vector.memset(sq_win[t][:, S:], 0.0)
+            nc.vector.memset(lookup[t][:, S:], 0.0)
 
         tok_bytes = sb.tile([P, S], U8, name="tok_bytes", align_bytes=64)
         nc.vector.tensor_copy(tok_bytes[:], table_bytes[:].indirect(offs_t[:]))
@@ -74,7 +85,7 @@ def tile_picked_candrmscube_none_p_kernel(tc, x_words, x_scales, w1, gs, offs, n
         w16 = sb.tile([P, PACK, P, PACK], BF16, name="w16", align_bytes=64)
         for h in range(2):
             nc.scalar.copy(
-                w16[:, :, 64 * h : 64 * (h + 1), :].rearrange("p t m j -> p m t j"),
+                w16[:, :, h * P // 2 : (h + 1) * P // 2, :].rearrange("p t m j -> p m t j"),
                 w_raw[h][:].rearrange("p j (m t) -> p m t j", t=PACK),
             )
         w_words = sb.tile([P, H], U32, name="w_words", tag="table_bytes", align_bytes=64)
@@ -85,17 +96,26 @@ def tile_picked_candrmscube_none_p_kernel(tc, x_words, x_scales, w1, gs, offs, n
         for cols, entries in halves:
             nc.vector.tensor_copy(tok_words[:, cols], table_words[:].indirect(offs_t[:, entries]))
 
-        def product(name, tags, t, lhs_words, lhs_bytes, rhs_words, rhs_bytes):
+        def product(name, banks, t, lhs_words, lhs_bytes, rhs_words, rhs_bytes):
             rows = slice(t * P, (t + 1) * P)
             made = []
-            for tag, (cols, entries) in zip(tags, halves if len(tags) == 2 else whole):
+            for tag, (cols, entries) in zip(banks, halves if len(banks) == 2 else whole):
                 bank = ps.tile([P, cols.stop - cols.start], F32, name=f"{name}_{tag}", tag=tag)
-                nc.tensor.matmul_mx(bank[:], lhsT=lhs_words[:, rows].bitcast(FP8X4), lhsT_scale=lhs_bytes[:, rows], rhs=rhs_words[:, cols].bitcast(FP8X4), rhs_scale=rhs_bytes[:, cols], start=True, stop=True)
+                nc.tensor.matmul_mx(
+                    bank[:],
+                    lhsT=lhs_words[:, rows].bitcast(FP8X4),
+                    lhsT_scale=lhs_bytes[:, rows],
+                    rhs=rhs_words[:, cols].bitcast(FP8X4),
+                    rhs_scale=rhs_bytes[:, cols],
+                    start=True,
+                    stop=True,
+                )
                 made.append((bank, cols))
             return made
 
         bank_tags = [["bank0a", "bank0b"], ["bank1"], ["bank2"], ["bank3"]]
         y_ps = [product("y", bank_tags[t], t, w_words, w_bytes, tok_words, tok_bytes) for t in range(PACK)]
+
         cand_bytes = sb.tile([P, C], U8, name="cand_bytes", align_bytes=64)
         nc.vector.tensor_copy(
             cand_bytes[:].rearrange("p (t m) -> p m t", t=PACK),
@@ -104,49 +124,33 @@ def tile_picked_candrmscube_none_p_kernel(tc, x_words, x_scales, w1, gs, offs, n
         cand_words = sb.tile([P, C], U32, name="cand_words", align_bytes=64)
         nc.vector.tensor_copy(cand_words[:].rearrange("p (t m) -> p m t", t=PACK), table_words[:].indirect(cand_t[:]))
 
-        den = [sb.tile([P, S], F32, name=f"den{t}") for t in range(PACK)]
-        inv = [sb.tile([P, S], F32, name=f"inv{t}") for t in range(PACK)]
+        sq_sum = [sb.tile([P, S], F32, name=f"sq_sum{t}") for t in range(PACK)]
+        inv_root = [sb.tile([P, S], F32, name=f"inv_root{t}") for t in range(PACK)]
         z32 = sb.tile([P, PACK, S], F32, name="z32")
 
-        def squares(t):
-            for bank, cols in y_ps[t]:
-                nc.scalar.activation(sq_win[t][:, cols], bank[:], ACT.Square)
-                nc.scalar.activation(y_win[t][:, S + cols.start : S + cols.stop], bank[:], ACT.Square)
-
-        def gained(t):
-            for bank, cols in y_ps[t]:
-                nc.scalar.activation(y_win[t][:, cols], bank[:], ACT.Copy, scale=gs_t[:, t : t + 1])
-
         def add_squares(t, pieces):
+            for bank, cols in y_ps[t]:
+                nc.scalar.activation(lookup[t][:, cols], bank[:], ACT.Square)
+                nc.scalar.activation(y_and_sq[t][:, S + cols.start : S + cols.stop], bank[:], ACT.Square)
             for cols, entries in pieces:
-                nc.vector.tensor_tensor(den[t][:, cols], sq_win[t][:].indirect(n1_t[:, entries]), y_win[t][:, S + cols.start : S + cols.stop], ALU.add)
+                own = y_and_sq[t][:, S + cols.start : S + cols.stop]
+                nc.vector.tensor_tensor(sq_sum[t][:, cols], lookup[t][:].indirect(n1_t[:, entries]), own, ALU.add)
 
-        def inverse_root(t):
-            nc.scalar.activation(inv[t][:], den[t][:], ACT.Abs_reciprocal_sqrt, bias=quarter[:])
+        def factors(t):
+            for bank, cols in y_ps[t]:
+                nc.scalar.activation(y_and_sq[t][:, cols], bank[:], ACT.Copy, scale=gs_t[:, t : t + 1])
+            nc.scalar.activation(inv_root[t][:], sq_sum[t][:], ACT.Abs_reciprocal_sqrt, bias=quarter[:])
 
         def normalise(t, pieces):
             for cols, entries in pieces:
-                nc.vector.tensor_tensor(z32[:, t, cols], y_win[t][:].indirect(n2_t[:, entries]), inv[t][:, cols], ALU.mult)
+                nc.vector.tensor_tensor(z32[:, t, cols], y_and_sq[t][:].indirect(n2_t[:, entries]), inv_root[t][:, cols], ALU.mult)
 
-        squares(0)
         add_squares(0, halves)
-        squares(1)
-        add_squares(1, whole)
-        gained(0)
-        inverse_root(0)
-        normalise(0, whole)
-        squares(2)
-        add_squares(2, whole)
-        inverse_root(1)
-        gained(1)
-        normalise(1, whole)
-        squares(3)
-        add_squares(3, whole)
-        inverse_root(2)
-        gained(2)
-        normalise(2, whole)
-        gained(3)
-        inverse_root(3)
+        for t in range(last):
+            add_squares(t + 1, whole)
+            factors(t)
+            normalise(t, whole)
+        factors(last)
 
         z16 = [sb.tile([P, HALF, PACK], BF16, name=f"z16_{h}", align_bytes=64) for h in range(2)]
         z_words = sb.tile([P, S], U32, name="z_words", align_bytes=64)
@@ -155,57 +159,53 @@ def tile_picked_candrmscube_none_p_kernel(tc, x_words, x_scales, w1, gs, offs, n
         def interleave(copy, h):
             copy(
                 z16[h][:].rearrange("p (c i) t -> p c t i", i=4),
-                z32[:, :, h * HALF : (h + 1) * HALF].rearrange("p t (c i) -> p c t i", i=4),
+                z32[:, :, halves[h][0]].rearrange("p t (c i) -> p c t i", i=4),
             )
 
-        def quantise(h):
-            nc.vector.quantize_mx(z_words[:, halves[h][0]].bitcast(FP8X4), z_bytes[:, halves[h][0]], z16[h][:].rearrange("p c t -> p (c t)"))
-
-        normalise(3, halves[:1])
+        normalise(last, halves[:1])
         interleave(nc.scalar.copy, 0)
-        normalise(3, halves[1:])
+        normalise(last, halves[1:])
         interleave(nc.vector.tensor_copy, 1)
-        quantise(0)
-        quantise(1)
+        for h, (cols, entries) in enumerate(halves):
+            nc.vector.quantize_mx(z_words[:, cols].bitcast(FP8X4), z_bytes[:, cols], z16[h][:].rearrange("p c t -> p (c t)"))
 
-        def score(t, tags):
-            return product("s", tags, t, cand_words, cand_bytes, z_words, z_bytes)
+        def score(t, banks):
+            return product("s", banks, t, cand_words, cand_bytes, z_words, z_bytes)
 
-        s_ps = [score(t, bank_tags[t]) for t in range(PACK - 1)]
-
+        raw_ps = [score(t, bank_tags[t]) for t in range(last)]
         out_rows = out.rearrange("(p t) n -> t p n", t=PACK)
-        s_win = sq_win
         sig = [sb.tile([P, S], F32, name=f"sig{t}") for t in range(PACK)]
-        prod = [sb.tile([P, S], F32, name=f"prod{t}") for t in range(PACK)]
-        res = [sb.tile([P, S], F32, name=f"res{t}") for t in range(PACK)]
+        gated = [sb.tile([P, S], F32, name=f"gated{t}") for t in range(PACK)]
+        result = [sb.tile([P, S], F32, name=f"result{t}") for t in range(PACK)]
 
         def sigmoid(t, pieces):
             for cols, entries in pieces:
-                nc.scalar.activation(sig[t][:, cols], s_win[t][:].indirect(n4_t[:, entries]), ACT.Sigmoid, scale=16.0)
+                nc.scalar.activation(sig[t][:, cols], lookup[t][:].indirect(n4_t[:, entries]), ACT.Sigmoid, scale=SIGMOID_SCALE)
 
         def gate(t):
-            for bank, cols in s_ps[t]:
-                nc.vector.scalar_tensor_tensor(prod[t][:, cols], sig[t][:, cols], 0.5, bank[:], ALU.subtract, ALU.mult)
+            for bank, cols in raw_ps[t]:
+                nc.vector.scalar_tensor_tensor(gated[t][:, cols], sig[t][:, cols], 0.5, bank[:], ALU.subtract, ALU.mult)
 
         def finish(t, pieces):
             for cols, entries in pieces:
-                nc.vector.tensor_tensor(res[t][:, cols], s_win[t][:].indirect(n3_t[:, entries]), prod[t][:, cols], ALU.mult)
-                nc.sync.dma_start(out_rows[t][:, cols], res[t][:, cols])
+                nc.vector.tensor_tensor(result[t][:, cols], lookup[t][:].indirect(n3_t[:, entries]), gated[t][:, cols], ALU.mult)
+                nc.sync.dma_start(out_rows[t][:, cols], result[t][:, cols])
 
-        for t in range(PACK - 1):
-            for bank, cols in s_ps[t]:
-                nc.vector.tensor_scalar(s_win[t][:, cols], bank[:], 1.0 / 128, None, ALU.mult)
+        for t in range(last):
+            for bank, cols in raw_ps[t]:
+                nc.vector.tensor_scalar(lookup[t][:, cols], bank[:], WINDOW_SCALE, None, ALU.mult)
         sigmoid(0, halves)
         gate(0)
-        s_ps.append(score(3, ["bank0b"]))
+        raw_ps.append(score(last, ["bank0b"]))
         finish(0, halves)
         sigmoid(1, whole)
         gate(1)
         sigmoid(2, whole)
         gate(2)
         finish(1, whole)
-        nc.scalar.activation(s_win[3][:, :S], s_ps[3][0][0][:], ACT.Copy, scale=1.0 / 128)
-        sigmoid(3, whole)
-        gate(3)
+        last_bank, last_cols = raw_ps[last][0]
+        nc.scalar.activation(lookup[last][:, last_cols], last_bank[:], ACT.Copy, scale=WINDOW_SCALE)
+        sigmoid(last, whole)
+        gate(last)
         finish(2, whole)
-        finish(3, [(slice(0, 384), slice(0, 24)), (slice(384, 512), slice(24, 32))])
+        finish(last, [piece(0, S - LAST_PIECE), piece(S - LAST_PIECE, S)])

from contextlib import ExitStack

import concourse.mybir as mybir

K, T, S, H, C = 512, 2048, 512, 512, 512
FLOPS = 2 * K * H * S + 2 * K * C * S

F32 = mybir.dt.float32
BF16 = mybir.dt.bfloat16
I32 = mybir.dt.int32
U32 = mybir.dt.uint32
U16 = mybir.dt.uint16
U8 = mybir.dt.uint8
FP8X4 = mybir.dt.float8_e4m3fn_x4
ACT = mybir.ActivationFunctionType
ALU = mybir.AluOpType

P = 128
PACK = 4
PER_COLUMN = 16
HALF = S // 2
LAST_PIECE = 128

SCORE_SCALE = 0.0625
WINDOW_SCALE = 2 * SCORE_SCALE * SCORE_SCALE
SIGMOID_SCALE = 2 * SCORE_SCALE / WINDOW_SCALE


def piece(start, stop):
    return slice(start, stop), slice(start // PER_COLUMN, stop // PER_COLUMN)


def tile_picked_candrmscube_none_p_kernel(tc, x_words, x_scales, w1, gs, offs, n1, n2, cand, n3, n4, out):
    nc = tc.nc
    whole = [piece(0, S)]
    halves = [piece(0, HALF), piece(HALF, S)]
    last = PACK - 1

    with ExitStack() as ctx:
        lists = ctx.enter_context(tc.tile_pool(name="lists", bufs=1))
        sb = ctx.enter_context(tc.tile_pool(name="sb", bufs=1))
        ps = ctx.enter_context(tc.psum_pool(name="ps", bufs=1))

        def load_list(name, src):
            tile = lists.tile([P, S // PER_COLUMN], U16, name=name)
            nc.sync.dma_start(tile[:], src)
            return tile

        table_bytes = sb.tile([P, T], U8, name="table_bytes", tag="table_bytes", align_bytes=64)
        nc.vector.memset(table_bytes[:, : T // 2].bitcast(I32), 0)
        nc.gpsimd.memset(table_bytes[:, T // 2 :].bitcast(I32), 0)

        w_rows = w1.rearrange("(p j) c -> p j c", j=PACK)
        w_raw = [sb.tile([P, PACK, H // 2], F32, name=f"w_raw{h}") for h in range(2)]
        offs_t = load_list("offs_t", offs)
        nc.sync.dma_start(w_raw[0][:], w_rows[:, :, : H // 2])
        cand_t = load_list("cand_t", cand)
        n1_t = load_list("n1_t", n1)
        for q in range(P // 32):
            nc.sync.dma_start(table_bytes[32 * q : 32 * q + 4, :].bitcast(I32), x_scales[0, 4 * q : 4 * q + 4, :].bitcast(I32))
        nc.sync.dma_start(w_raw[1][:], w_rows[:, :, H // 2 :])
        table_words = sb.tile([P, T], U32, name="table_words")
        nc.sync.dma_start(table_words[:].bitcast(I32), x_words[0].rearrange("p n r -> p (n r)").bitcast(I32))
        n2_t = load_list("n2_t", n2)
        n3_t = load_list("n3_t", n3)
        n4_t = load_list("n4_t", n4)
        gs_t = sb.tile([P, PACK], F32, name="gs_t")
        nc.sync.dma_start(gs_t[:], gs.rearrange("(p t) o -> p (t o)", t=PACK))

        sixteen = sb.tile([P, 1], F32, name="sixteen")
        nc.vector.memset(sixteen[:], 16.0)
        quarter = sb.tile([P, 1], F32, name="quarter")
        nc.scalar.activation(quarter[:], sixteen[:], ACT.Abs_reciprocal_sqrt)

        y_and_sq = [sb.tile([P, 2 * S], F32, name=f"y_and_sq{t}") for t in range(PACK)]
        lookup = [sb.tile([P, 2 * S], F32, name=f"lookup{t}") for t in range(PACK)]
        for t in range(PACK):
            nc.vector.memset(lookup[t][:, S:], 0.0)

        tok_bytes = sb.tile([P, S], U8, name="tok_bytes", align_bytes=64)
        nc.vector.tensor_copy(tok_bytes[:], table_bytes[:].indirect(offs_t[:]))
        cand_bytes_listed = sb.tile([P, C], U8, name="cand_bytes_listed")
        nc.vector.tensor_copy(cand_bytes_listed[:], table_bytes[:].indirect(cand_t[:]))

        w16 = sb.tile([P, PACK, P, PACK], BF16, name="w16", align_bytes=64)
        for h in range(2):
            nc.scalar.copy(
                w16[:, :, h * P // 2 : (h + 1) * P // 2, :].rearrange("p t m j -> p m t j"),
                w_raw[h][:].rearrange("p j (m t) -> p m t j", t=PACK),
            )
        w_words = sb.tile([P, H], U32, name="w_words", tag="table_bytes", align_bytes=64)
        w_bytes = sb.tile([P, H], U8, name="w_bytes", align_bytes=64)
        nc.vector.quantize_mx(w_words[:].bitcast(FP8X4), w_bytes[:], w16[:].rearrange("p t m j -> p (t m j)"))

        tok_words = sb.tile([P, S], U32, name="tok_words", align_bytes=64)
        for cols, entries in halves:
            nc.vector.tensor_copy(tok_words[:, cols], table_words[:].indirect(offs_t[:, entries]))

        def product(name, banks, t, lhs_words, lhs_bytes, rhs_words, rhs_bytes):
            rows = slice(t * P, (t + 1) * P)
            made = []
            for tag, (cols, entries) in zip(banks, halves if len(banks) == 2 else whole):
                bank = ps.tile([P, cols.stop - cols.start], F32, name=f"{name}_{tag}", tag=tag)
                nc.tensor.matmul_mx(
                    bank[:],
                    lhsT=lhs_words[:, rows].bitcast(FP8X4),
                    lhsT_scale=lhs_bytes[:, rows],
                    rhs=rhs_words[:, cols].bitcast(FP8X4),
                    rhs_scale=rhs_bytes[:, cols],
                    start=True,
                    stop=True,
                )
                made.append((bank, cols))
            return made

        bank_tags = [["bank0a", "bank0b"], ["bank1"], ["bank2"], ["bank3"]]
        y_ps = [product("y", bank_tags[t], t, w_words, w_bytes, tok_words, tok_bytes) for t in range(PACK)]

        cand_bytes = sb.tile([P, C], U8, name="cand_bytes", align_bytes=64)
        nc.vector.tensor_copy(
            cand_bytes[:].rearrange("p (t m) -> p m t", t=PACK),
            cand_bytes_listed[:].rearrange("p (m t) -> p m t", t=PACK),
        )
        cand_words = sb.tile([P, C], U32, name="cand_words", align_bytes=64)
        nc.vector.tensor_copy(cand_words[:].rearrange("p (t m) -> p m t", t=PACK), table_words[:].indirect(cand_t[:]))

        sq_sum = [sb.tile([P, S], F32, name=f"sq_sum{t}") for t in range(PACK)]
        inv_root = [sb.tile([P, S], F32, name=f"inv_root{t}") for t in range(PACK)]
        z32 = sb.tile([P, PACK, S], F32, name="z32")

        def add_squares(t, pieces):
            for bank, cols in y_ps[t]:
                nc.scalar.activation(lookup[t][:, cols], bank[:], ACT.Square)
                nc.scalar.activation(y_and_sq[t][:, S + cols.start : S + cols.stop], bank[:], ACT.Square)
            for cols, entries in pieces:
                own = y_and_sq[t][:, S + cols.start : S + cols.stop]
                nc.vector.tensor_tensor(sq_sum[t][:, cols], lookup[t][:].indirect(n1_t[:, entries]), own, ALU.add)

        def factors(t):
            for bank, cols in y_ps[t]:
                nc.scalar.activation(y_and_sq[t][:, cols], bank[:], ACT.Copy, scale=gs_t[:, t : t + 1])
            nc.scalar.activation(inv_root[t][:], sq_sum[t][:], ACT.Abs_reciprocal_sqrt, bias=quarter[:])

        def normalise(t, pieces):
            for cols, entries in pieces:
                nc.vector.tensor_tensor(z32[:, t, cols], y_and_sq[t][:].indirect(n2_t[:, entries]), inv_root[t][:, cols], ALU.mult)

        add_squares(0, halves)
        for t in range(last):
            add_squares(t + 1, whole)
            factors(t)
            normalise(t, whole)
        factors(last)

        z16 = [sb.tile([P, HALF, PACK], BF16, name=f"z16_{h}", align_bytes=64) for h in range(2)]
        z_words = sb.tile([P, S], U32, name="z_words", align_bytes=64)
        z_bytes = sb.tile([P, S], U8, name="z_bytes", align_bytes=64)

        def interleave(copy, h):
            copy(
                z16[h][:].rearrange("p (c i) t -> p c t i", i=4),
                z32[:, :, halves[h][0]].rearrange("p t (c i) -> p c t i", i=4),
            )

        normalise(last, halves[:1])
        interleave(nc.scalar.copy, 0)
        normalise(last, halves[1:])
        interleave(nc.vector.tensor_copy, 1)
        for h, (cols, entries) in enumerate(halves):
            nc.vector.quantize_mx(z_words[:, cols].bitcast(FP8X4), z_bytes[:, cols], z16[h][:].rearrange("p c t -> p (c t)"))

        def score(t, banks):
            return product("s", banks, t, cand_words, cand_bytes, z_words, z_bytes)

        raw_ps = [score(t, bank_tags[t]) for t in range(last)]
        out_rows = out.rearrange("(p t) n -> t p n", t=PACK)
        sig = [sb.tile([P, S], F32, name=f"sig{t}") for t in range(PACK)]
        gated = [sb.tile([P, S], F32, name=f"gated{t}") for t in range(PACK)]
        result = [sb.tile([P, S], F32, name=f"result{t}") for t in range(PACK)]

        def sigmoid(t, pieces):
            for cols, entries in pieces:
                nc.scalar.activation(sig[t][:, cols], lookup[t][:].indirect(n4_t[:, entries]), ACT.Sigmoid, scale=SIGMOID_SCALE)

        def gate(t):
            for bank, cols in raw_ps[t]:
                nc.vector.scalar_tensor_tensor(gated[t][:, cols], sig[t][:, cols], 0.5, bank[:], ALU.subtract, ALU.mult)

        def finish(t, pieces):
            for cols, entries in pieces:
                nc.vector.tensor_tensor(result[t][:, cols], lookup[t][:].indirect(n3_t[:, entries]), gated[t][:, cols], ALU.mult)
                nc.sync.dma_start(out_rows[t][:, cols], result[t][:, cols])

        for t in range(last):
            for bank, cols in raw_ps[t]:
                nc.vector.tensor_scalar(lookup[t][:, cols], bank[:], WINDOW_SCALE, None, ALU.mult)
        sigmoid(0, halves)
        gate(0)
        raw_ps.append(score(last, ["bank0b"]))
        finish(0, halves)
        sigmoid(1, whole)
        gate(1)
        sigmoid(2, whole)
        gate(2)
        finish(1, whole)
        last_bank, last_cols = raw_ps[last][0]
        nc.scalar.activation(lookup[last][:, last_cols], last_bank[:], ACT.Copy, scale=WINDOW_SCALE)
        sigmoid(last, whole)
        gate(last)
        finish(2, whole)
        finish(last, [piece(0, S - LAST_PIECE), piece(S - LAST_PIECE, S)])
